import numpy as np
import ml_dtypes


def mxq(x, axis, fmt="e4m3"):
    dtype, down = {"e4m3": (ml_dtypes.float8_e4m3fn, 7), "e5m2": (ml_dtypes.float8_e5m2, 14)}[fmt]
    v = np.moveaxis(np.asarray(x, np.float32).astype(ml_dtypes.bfloat16).astype(np.float64), axis, -1)
    blocks = v.reshape(v.shape[:-1] + (-1, 32))
    amax = np.abs(blocks).max(-1, keepdims=True)
    byte = np.maximum(np.where(amax > 0, np.frexp(amax)[1] - 1 + 127, 0) - down, 1)
    scale = np.exp2(byte - 127.0)
    codes = (blocks / scale).astype(np.float32).astype(dtype).astype(np.float64)
    return np.moveaxis((codes * scale).reshape(v.shape), -1, axis)


WIDE = False


def mx_kscale(k):
    if not WIDE:
        return np.ones(k)
    levels = np.array([10, -10, 5, -5, 0])
    if k % 512:
        return np.exp2(np.random.permutation(np.resize(levels, k // 32))).repeat(32)
    a = np.empty((k // 512, 16))
    for p in range(k // 512):
        a[p, :8] = np.random.permutation(np.resize(levels, 8))
        for g in range(8):
            far = levels[np.abs(levels - a[p, g]) >= 10]
            a[p, g + 8] = far[np.random.randint(len(far))]
    return np.exp2(a.ravel()).repeat(32)


def f64(x):
    return np.asarray(x).astype(np.float64)


E2M1 = np.array([0.0, 0.5, 1.0, 1.5, 2.0, 3.0, 4.0, 6.0, -0.0, -0.5, -1.0, -1.5, -2.0, -3.0, -4.0, -6.0])


def pack_weight(w, fmt):
    k, n = w.shape
    w = f64(np.asarray(w, np.float32).astype(ml_dtypes.bfloat16)).reshape(k // 32, 32, n)
    amax = np.abs(w).max(1)
    if fmt == "e4m3":
        byte = np.frexp(amax)[1] - 1 + 127 - 7
    else:
        mant, ex = np.frexp(amax / 6.0)
        byte = np.where(mant > 0.5, ex, ex - 1) + 127
    byte = np.clip(np.where(amax > 0, byte, 1), 1, 254)
    scaled = (w * np.exp2(127.0 - byte)[:, None, :]).reshape(k, n).astype(np.float32)
    by_word = np.ascontiguousarray(scaled.reshape(k // 512, 128, 4, n).transpose(0, 1, 3, 2))
    if fmt == "e4m3":
        words = by_word.astype(ml_dtypes.float8_e4m3fn).view(np.uint8)
    else:
        c = by_word.astype(ml_dtypes.float4_e2m1fn).view(np.uint8) & 0xF
        words = (c[..., 0::2] | (c[..., 1::2] << 4)).reshape(k // 512, 128, 2 * n)
    return np.ascontiguousarray(words), np.ascontiguousarray(byte.astype(np.uint8).reshape(k // 512, 16, n))


def unpack_weight(words, scales, fmt):
    g, _, n = scales.shape
    words = np.ascontiguousarray(words).reshape(g, 128, n, -1)
    if fmt == "e4m3":
        vals = words.view(ml_dtypes.float8_e4m3fn).astype(np.float64)
    else:
        nib = np.empty((g, 128, n, 4), np.uint8)
        nib[..., 0::2] = words & 0xF
        nib[..., 1::2] = words >> 4
        vals = E2M1[nib]
    vals = vals * np.repeat(np.exp2(scales.astype(np.float64) - 127.0), 8, axis=1)[..., None]
    return vals.transpose(0, 1, 3, 2).reshape(g * 512, n)


K, L, T, N = 1024, 1024, 512, 512


def setup_inputs():
    n = np.random.standard_normal
    fk = mx_kscale(K)
    fl = mx_kscale(L)
    xtp = pack_weight(n((K, T)) / fk[:, None], "e4m3")
    xqp = pack_weight(n((L, T)) / fl[:, None], "e2m1")
    wqp = pack_weight(n((L, N)) * 1 / np.sqrt(L) * fl[:, None], "e4m3")
    wdp = pack_weight(n((K, N)) * 1 / np.sqrt(K) * fk[:, None], "e2m1")
    return {
        "xt_words": xtp[0],
        "xt_scales": xtp[1],
        "wa": (n((K, N)) * 1 / np.sqrt(K) * fk[:, None]).astype(np.float32),
        "xq_words": xqp[0],
        "xq_scales": xqp[1],
        "wq_words": wqp[0],
        "wq_scales": wqp[1],
        "wd_words": wdp[0],
        "wd_scales": wdp[1],
        "sh": (np.random.uniform(0.1, 0.4, (N, 1))).astype(np.float32),
    }


def reference(xt_words, xt_scales, wa, xq_words, xq_scales, wq_words, wq_scales, wd_words, wd_scales, sh):
    xtu = unpack_weight(xt_words, xt_scales, "e4m3")
    xqu = unpack_weight(xq_words, xq_scales, "e2m1")
    wqu = unpack_weight(wq_words, wq_scales, "e4m3")
    wdu = unpack_weight(wd_words, wd_scales, "e2m1")
    waq = mxq(f64(wa), 0, "e4m3")
    p = waq.T @ xtu + wqu.T @ xqu
    d = wdu.T @ xtu
    y = p / (1.0 + np.maximum(d, 0.0)) + f64(sh) * d
    return y

@@ -1,0 +1,210 @@
+from contextlib import ExitStack
+
+import concourse.mybir as mybir
+
+K, L, T, N = 1024, 1024, 512, 512
+FLOPS = 2 * N * T * (K + L + K)
+
+F32 = mybir.dt.float32
+BF16 = mybir.dt.bfloat16
+I32 = mybir.dt.int32
+U32 = mybir.dt.uint32
+U8 = mybir.dt.uint8
+FP8X4 = mybir.dt.float8_e4m3fn_x4
+FP4X4 = mybir.dt.float4_e2m1fn_x4
+ACT = mybir.ActivationFunctionType
+ALU = mybir.AluOpType
+
+P = 128
+PACK = 4
+PASSES = 2
+TILES = N // P
+HALF = N // 2
+
+
+def tile_mix_sum_divided_by_drive_kernel(
+    tc, xt_words, xt_scales, wa, xq_words, xq_scales, wq_words, wq_scales, wd_words, wd_scales, sh, out
+):
+    nc = tc.nc
+    with ExitStack() as ctx:
+        keep = ctx.enter_context(tc.tile_pool(name="keep", bufs=1))
+        psum = ctx.enter_context(tc.psum_pool(name="psum", bufs=1))
+        ctx.enter_context(tc.manual_schedule())
+
+        xt_w = keep.tile([P, PASSES, T], U32, align_bytes=64)
+        wq_w = keep.tile([P, PASSES, N], U32, align_bytes=64)
+        xq_w = keep.tile([P, PASSES, 2 * T], U8, align_bytes=64)
+        wd_w = keep.tile([P, PASSES, 2 * N], U8, align_bytes=64)
+        xt_s = keep.tile([P, PASSES, T], U8, align_bytes=64)
+        xq_s = keep.tile([P, PASSES, T], U8, align_bytes=64)
+        wq_s = keep.tile([P, PASSES, N], U8, align_bytes=64)
+        wd_s = keep.tile([P, PASSES, N], U8, align_bytes=64)
+        sh_sb = keep.tile([P, TILES], F32)
+        one = keep.tile([P, 1], F32)
+        warm = keep.tile([P, 1], F32)
+
+        chunks = [(z, h) for h in range(2) for z in range(PASSES)]
+        raw, grouped, wa_w, wa_s = {}, {}, {}, {}
+        for z, h in chunks:
+            raw[z, h] = keep.tile([P, PACK, HALF], F32, name="raw%d%d" % (z, h))
+            grouped[z, h] = keep.tile([P, HALF, PACK], BF16, name="grouped%d%d" % (z, h), align_bytes=64)
+            wa_w[z, h] = keep.tile([P, HALF], U32, name="wa_w%d%d" % (z, h), align_bytes=64)
+            wa_s[z, h] = keep.tile([P, HALF], U8, name="wa_s%d%d" % (z, h), align_bytes=64)
+        drive = [psum.tile([P, T], F32, name="drive%d" % i) for i in range(TILES)]
+        total = [psum.tile([P, T], F32, name="total%d" % i) for i in range(TILES)]
+        pos = [keep.tile([P, T], F32, name="pos%d" % i) for i in range(TILES)]
+        root = [keep.tile([P, T], F32, name="root%d" % i) for i in range(TILES)]
+        recip = [keep.tile([P, T], F32, name="recip%d" % i) for i in range(TILES)]
+        quot = [keep.tile([P, T], F32, name="quot%d" % i) for i in range(TILES)]
+        res = [keep.tile([P, T], F32, name="res%d" % i) for i in range(TILES)]
+
+        def zero(eng, plane):
+            eng.memset(plane[:].rearrange("p z c -> p (z c)").bitcast(I32), 0)
+
+        def load_scales(eng, plane, scales):
+            rows = scales.rearrange("z (q r) c -> r q z c", r=4)
+            for r in range(4):
+                eng.dma_start(out=plane[r:P:32, :, :].bitcast(I32), in_=rows[r].bitcast(I32))
+
+        def load_fp8(dst, words):
+            nc.sync.dma_start(out=dst[:].bitcast(I32), in_=words.rearrange("z p c r -> p z (c r)").bitcast(I32))
+
+        def load_fp4(dst, words):
+            nc.sync.dma_start(out=dst[:].bitcast(I32), in_=words.rearrange("z p c -> p z c").bitcast(I32))
+
+        def load_wa(z, h):
+            rows = wa[z * 512 : (z + 1) * 512, h * HALF : (h + 1) * HALF]
+            nc.sync.dma_start(out=raw[z, h][:], in_=rows.rearrange("(p j) c -> p j c", j=PACK))
+
+        def cast(z, h):
+            nc.vector.tensor_copy(
+                out=grouped[z, h][:].rearrange("p (c i) j -> p c j i", i=4),
+                in_=raw[z, h][:].rearrange("p j (c i) -> p c j i", i=4),
+            )
+
+        def quantise(z, h):
+            nc.vector.quantize_mx(
+                out=wa_w[z, h][:].bitcast(FP8X4),
+                scales=wa_s[z, h][:],
+                in_=grouped[z, h][:].rearrange("p c j -> p (c j)"),
+            )
+
+        def drive_pass(i, z):
+            nc.tensor.matmul_mx(
+                out=drive[i][:],
+                lhsT=wd_w[:, z, 2 * P * i : 2 * P * (i + 1)].bitcast(FP4X4),
+                lhsT_scale=wd_s[:, z, P * i : P * (i + 1)],
+                rhs=xt_w[:, z, :].bitcast(FP8X4),
+                rhs_scale=xt_s[:, z, :],
+                start=(z == 0),
+                stop=(z == PASSES - 1),
+            )
+
+        def wa_pass(i, z, start, stop):
+            h, c = divmod(i * P, HALF)
+            nc.tensor.matmul_mx(
+                out=total[i][:],
+                lhsT=wa_w[z, h][:, c : c + P].bitcast(FP8X4),
+                lhsT_scale=wa_s[z, h][:, c : c + P],
+                rhs=xt_w[:, z, :].bitcast(FP8X4),
+                rhs_scale=xt_s[:, z, :],
+                start=start,
+                stop=stop,
+            )
+
+        def wq_pass(i, z, start, stop):
+            nc.tensor.matmul_mx(
+                out=total[i][:],
+                lhsT=wq_w[:, z, P * i : P * (i + 1)].bitcast(FP8X4),
+                lhsT_scale=wq_s[:, z, P * i : P * (i + 1)],
+                rhs=xq_w[:, z, :].bitcast(FP4X4),
+                rhs_scale=xq_s[:, z, :],
+                start=start,
+                stop=stop,
+            )
+
+        def positive(i):
+            nc.scalar.activation(out=pos[i][:], in_=drive[i][:], func=ACT.Relu)
+
+        def inv_root(i):
+            nc.scalar.activation(out=root[i][:], in_=pos[i][:], func=ACT.Abs_reciprocal_sqrt, bias=1.0)
+
+        def square(i):
+            nc.scalar.activation(out=recip[i][:], in_=root[i][:], func=ACT.Square)
+
+        def divide(i):
+            nc.vector.tensor_tensor(out=quot[i][:], in0=total[i][:], in1=recip[i][:], op=ALU.mult)
+
+        def add_share(i):
+            nc.vector.scalar_tensor_tensor(
+                out=res[i][:], in0=drive[i][:], scalar=sh_sb[:, i : i + 1], in1=quot[i][:], op0=ALU.mult, op1=ALU.add
+            )
+
+        def store(i):
+            nc.sync.dma_start(out=out[P * i : P * (i + 1), :], in_=res[i][:])
+
+        zero(nc.vector, xt_s)
+        zero(nc.gpsimd, wd_s)
+        zero(nc.vector, xq_s)
+        zero(nc.vector, wq_s)
+        nc.vector.memset(one[:], 1.0)
+
+        load_scales(nc.scalar, xt_s, xt_scales)
+        load_fp8(xt_w, xt_words)
+        load_fp4(wd_w, wd_words)
+        load_wa(0, 0)
+        load_wa(1, 0)
+        load_scales(nc.gpsimd, wd_s, wd_scales)
+        nc.scalar.activation(out=warm[:], in_=one[:], func=ACT.Abs_reciprocal_sqrt)
+        load_scales(nc.sync, xq_s, xq_scales)
+        load_fp4(xq_w, xq_words)
+        load_fp8(wq_w, wq_words)
+        load_wa(0, 1)
+        load_wa(1, 1)
+        load_scales(nc.gpsimd, wq_s, wq_scales)
+        with nc.allow_non_contiguous_dma(reason="one share a partition"):
+            nc.sync.dma_start(out=sh_sb[:], in_=sh.rearrange("(i p) o -> p (i o)", p=P))
+
+        for i in range(TILES):
+            for z in range(PASSES):
+                drive_pass(i, z)
+
+        positive(0)
+        for i in range(TILES):
+            inv_root(i)
+            if i + 1 < TILES:
+                positive(i + 1)
+            square(i)
+
+        for z in range(PASSES):
+            cast(z, 0)
+            quantise(z, 0)
+            wa_pass(0, z, z == 0, False)
+            wa_pass(1, z, z == 0, False)
+        for i in (0, 1):
+            for z in range(PASSES):
+                wq_pass(i, z, False, z == PASSES - 1)
+        for i in (2, 3):
+            for z in range(PASSES):
+                wq_pass(i, z, z == 0, False)
+
+        cast(0, 1)
+        divide(0)
+        quantise(0, 1)
+        wa_pass(2, 0, False, False)
+        wa_pass(3, 0, False, False)
+        cast(1, 1)
+        add_share(0)
+        store(0)
+        quantise(1, 1)
+        wa_pass(2, 1, False, True)
+        wa_pass(3, 1, False, True)
+        divide(1)
+        divide(2)
+        add_share(1)
+        store(1)
+        divide(3)
+        add_share(2)
+        store(2)
+        add_share(3)
+        store(3)

@@ -35,13 +35,11 @@ def tile_mix_sum_divided_by_drive_kernel(
         wq_w = keep.tile([P, PASSES, N], U32, align_bytes=64)
         xq_w = keep.tile([P, PASSES, 2 * T], U8, align_bytes=64)
         wd_w = keep.tile([P, PASSES, 2 * N], U8, align_bytes=64)
-        xt_s = keep.tile([P, PASSES, T], U8, align_bytes=64)
-        xq_s = keep.tile([P, PASSES, T], U8, align_bytes=64)
-        wq_s = keep.tile([P, PASSES, N], U8, align_bytes=64)
-        wd_s = keep.tile([P, PASSES, N], U8, align_bytes=64)
-        sh_sb = keep.tile([P, TILES], F32)
-        one = keep.tile([P, 1], F32)
-        warm = keep.tile([P, 1], F32)
+        staged = keep.tile([32, 4, PASSES, T], U8, align_bytes=64)
+        planes = keep.tile([P, 4, PASSES, T], U8, align_bytes=64)
+        xt_s, wd_s, xq_s, wq_s = (planes[:, a] for a in range(4))
+        sh_rows = keep.tile([P, P], F32, align_bytes=64)
+        sh_cols = keep.tile([P, P], F32, align_bytes=64)
 
         chunks = [(z, h) for h in range(2) for z in range(PASSES)]
         raw, grouped, wa_w, wa_s = {}, {}, {}, {}
@@ -58,23 +56,24 @@ def tile_mix_sum_divided_by_drive_kernel(
         quot = [keep.tile([P, T], F32, name="quot%d" % i) for i in range(TILES)]
         res = [keep.tile([P, T], F32, name="res%d" % i) for i in range(TILES)]
 
-        def zero(eng, plane):
-            eng.memset(plane[:].rearrange("p z c -> p (z c)").bitcast(I32), 0)
+        def stage_scales(eng, a, scales):
+            eng.dma_start(out=staged[16:32, a].bitcast(I32), in_=scales.rearrange("z q c -> q z c").bitcast(I32))
 
-        def load_scales(eng, plane, scales):
-            rows = scales.rearrange("z (q r) c -> r q z c", r=4)
-            for r in range(4):
-                eng.dma_start(out=plane[r:P:32, :, :].bitcast(I32), in_=rows[r].bitcast(I32))
+        def place_scales():
+            src = staged[:].rearrange("p a z c -> p (a z c)").bitcast(I32)
+            dst = planes[:].rearrange("p a z c -> p (a z c)").bitcast(I32)
+            for q in range(4):
+                nc.sync.dma_start(out=dst[32 * q : 32 * q + 4, :], in_=src[16 + 4 * q : 16 + 4 * q + 4, :])
 
-        def load_fp8(dst, words):
-            nc.sync.dma_start(out=dst[:].bitcast(I32), in_=words.rearrange("z p c r -> p z (c r)").bitcast(I32))
+        def load_fp8(eng, dst, words):
+            eng.dma_start(out=dst[:].bitcast(I32), in_=words.rearrange("z p c r -> p z (c r)").bitcast(I32))
 
-        def load_fp4(dst, words):
-            nc.sync.dma_start(out=dst[:].bitcast(I32), in_=words.rearrange("z p c -> p z c").bitcast(I32))
+        def load_fp4(eng, dst, words):
+            eng.dma_start(out=dst[:].bitcast(I32), in_=words.rearrange("z p c -> p z c").bitcast(I32))
 
-        def load_wa(z, h):
+        def load_wa(eng, z, h):
             rows = wa[z * 512 : (z + 1) * 512, h * HALF : (h + 1) * HALF]
-            nc.sync.dma_start(out=raw[z, h][:], in_=rows.rearrange("(p j) c -> p j c", j=PACK))
+            eng.dma_start(out=raw[z, h][:], in_=rows.rearrange("(p j) c -> p j c", j=PACK))
 
         def cast(z, h):
             nc.vector.tensor_copy(
@@ -126,6 +125,9 @@ def tile_mix_sum_divided_by_drive_kernel(
         def positive(i):
             nc.scalar.activation(out=pos[i][:], in_=drive[i][:], func=ACT.Relu)
 
+        def positive_v(i):
+            nc.vector.tensor_scalar(out=pos[i][:], in0=drive[i][:], scalar1=0.0, scalar2=None, op0=ALU.max)
+
         def inv_root(i):
             nc.scalar.activation(out=root[i][:], in_=pos[i][:], func=ACT.Abs_reciprocal_sqrt, bias=1.0)
 
@@ -137,72 +139,83 @@ def tile_mix_sum_divided_by_drive_kernel(
 
         def add_share(i):
             nc.vector.scalar_tensor_tensor(
-                out=res[i][:], in0=drive[i][:], scalar=sh_sb[:, i : i + 1], in1=quot[i][:], op0=ALU.mult, op1=ALU.add
+                out=res[i][:], in0=drive[i][:], scalar=sh_cols[:, 32 * i : 32 * i + 1], in1=quot[i][:], op0=ALU.mult, op1=ALU.add
             )
 
         def store(i):
             nc.sync.dma_start(out=out[P * i : P * (i + 1), :], in_=res[i][:])
 
-        zero(nc.vector, xt_s)
-        zero(nc.gpsimd, wd_s)
-        zero(nc.vector, xq_s)
-        zero(nc.vector, wq_s)
-        nc.vector.memset(one[:], 1.0)
+        nc.gpsimd.memset(sh_rows[:], 0.0)
+        nc.gpsimd.dma_start(
+            out=sh_rows[0:P:32, :].rearrange("a (i r) -> a i r", r=32),
+            in_=sh.rearrange("(i a r) o -> a i (r o)", a=4, r=32),
+        )
+        nc.vector.memset(planes[:].rearrange("p a z c -> p (a z c)").bitcast(I32), 0)
+        for a, scales in enumerate((xt_scales, wd_scales, xq_scales, wq_scales)):
+            stage_scales(nc.scalar if a % 2 else nc.sync, a, scales)
+        load_wa(nc.scalar, 0, 0)
+        load_fp8(nc.scalar, xt_w, xt_words)
+        load_fp4(nc.scalar, wd_w, wd_words)
+        load_wa(nc.scalar, 1, 0)
+        place_scales()
+        load_fp4(nc.sync, xq_w, xq_words)
+        load_fp8(nc.sync, wq_w, wq_words)
+        load_wa(nc.sync, 0, 1)
+        load_wa(nc.sync, 1, 1)
 
-        load_scales(nc.scalar, xt_s, xt_scales)
-        load_fp8(xt_w, xt_words)
-        load_fp4(wd_w, wd_words)
-        load_wa(0, 0)
-        load_wa(1, 0)
-        load_scales(nc.gpsimd, wd_s, wd_scales)
-        nc.scalar.activation(out=warm[:], in_=one[:], func=ACT.Abs_reciprocal_sqrt)
-        load_scales(nc.sync, xq_s, xq_scales)
-        load_fp4(xq_w, xq_words)
-        load_fp8(wq_w, wq_words)
-        load_wa(0, 1)
-        load_wa(1, 1)
-        load_scales(nc.gpsimd, wq_s, wq_scales)
-        with nc.allow_non_contiguous_dma(reason="one share a partition"):
-            nc.sync.dma_start(out=sh_sb[:], in_=sh.rearrange("(i p) o -> p (i o)", p=P))
-
-        for i in range(TILES):
+        def drive_tile(i):
             for z in range(PASSES):
                 drive_pass(i, z)
 
-        positive(0)
-        for i in range(TILES):
-            inv_root(i)
-            if i + 1 < TILES:
-                positive(i + 1)
-            square(i)
+        cast(0, 0)
+        quantise(0, 0)
+        nc.vector.transpose(out=sh_cols[:], in_=sh_rows[:])
 
-        for z in range(PASSES):
-            cast(z, 0)
-            quantise(z, 0)
-            wa_pass(0, z, z == 0, False)
-            wa_pass(1, z, z == 0, False)
-        for i in (0, 1):
-            for z in range(PASSES):
-                wq_pass(i, z, False, z == PASSES - 1)
+        drive_tile(0)
+        drive_tile(1)
+        positive_v(0)
+        inv_root(0)
+        positive(1)
+        square(0)
+        inv_root(1)
+        wa_pass(0, 0, True, False)
+        wa_pass(1, 0, True, False)
+        drive_tile(2)
+        positive(2)
+        square(1)
+        inv_root(2)
+        cast(1, 0)
+        quantise(1, 0)
+        wa_pass(0, 1, False, False)
+        wq_pass(0, 0, False, False)
+        wq_pass(0, 1, False, True)
+        drive_tile(3)
+        positive(3)
+        square(2)
+        inv_root(3)
+        square(3)
+        wa_pass(1, 1, False, False)
+        wq_pass(1, 0, False, False)
+        wq_pass(1, 1, False, True)
         for i in (2, 3):
             for z in range(PASSES):
                 wq_pass(i, z, z == 0, False)
 
-        cast(0, 1)
         divide(0)
+        cast(0, 1)
+        add_share(0)
+        store(0)
         quantise(0, 1)
         wa_pass(2, 0, False, False)
         wa_pass(3, 0, False, False)
         cast(1, 1)
-        add_share(0)
-        store(0)
+        divide(1)
         quantise(1, 1)
         wa_pass(2, 1, False, True)
         wa_pass(3, 1, False, True)
-        divide(1)
-        divide(2)
         add_share(1)
         store(1)
+        divide(2)
         divide(3)
         add_share(2)
         store(2)

@@ -62,8 +62,8 @@ def tile_mix_sum_divided_by_drive_kernel(
         def place_scales():
             src = staged[:].rearrange("p a z c -> p (a z c)").bitcast(I32)
             dst = planes[:].rearrange("p a z c -> p (a z c)").bitcast(I32)
-            for q in range(4):
-                nc.sync.dma_start(out=dst[32 * q : 32 * q + 4, :], in_=src[16 + 4 * q : 16 + 4 * q + 4, :])
+            for r in range(4):
+                nc.sync.dma_start(out=dst[r:P:32, :], in_=src[16 + r : 32 : 4, :])
 
         def load_fp8(eng, dst, words):
             eng.dma_start(out=dst[:].bitcast(I32), in_=words.rearrange("z p c r -> p z (c r)").bitcast(I32))
@@ -128,22 +128,27 @@ def tile_mix_sum_divided_by_drive_kernel(
         def positive_v(i):
             nc.vector.tensor_scalar(out=pos[i][:], in0=drive[i][:], scalar1=0.0, scalar2=None, op0=ALU.max)
 
-        def inv_root(i):
-            nc.scalar.activation(out=root[i][:], in_=pos[i][:], func=ACT.Abs_reciprocal_sqrt, bias=1.0)
+        def inv_root(i, cols=slice(0, T)):
+            nc.scalar.activation(out=root[i][:, cols], in_=pos[i][:, cols], func=ACT.Abs_reciprocal_sqrt, bias=1.0)
 
-        def square(i):
-            nc.scalar.activation(out=recip[i][:], in_=root[i][:], func=ACT.Square)
+        def square(i, cols=slice(0, T)):
+            nc.scalar.activation(out=recip[i][:, cols], in_=root[i][:, cols], func=ACT.Square)
 
-        def divide(i):
-            nc.vector.tensor_tensor(out=quot[i][:], in0=total[i][:], in1=recip[i][:], op=ALU.mult)
+        def divide(i, cols=slice(0, T)):
+            nc.vector.tensor_tensor(out=quot[i][:, cols], in0=total[i][:, cols], in1=recip[i][:, cols], op=ALU.mult)
 
-        def add_share(i):
+        def add_share(i, cols=slice(0, T)):
             nc.vector.scalar_tensor_tensor(
-                out=res[i][:], in0=drive[i][:], scalar=sh_cols[:, 32 * i : 32 * i + 1], in1=quot[i][:], op0=ALU.mult, op1=ALU.add
+                out=res[i][:, cols],
+                in0=drive[i][:, cols],
+                scalar=sh_cols[:, 32 * i : 32 * i + 1],
+                in1=quot[i][:, cols],
+                op0=ALU.mult,
+                op1=ALU.add,
             )
 
-        def store(i):
-            nc.sync.dma_start(out=out[P * i : P * (i + 1), :], in_=res[i][:])
+        def store(i, cols=slice(0, T)):
+            nc.sync.dma_start(out=out[P * i : P * (i + 1), cols], in_=res[i][:, cols])
 
         nc.gpsimd.memset(sh_rows[:], 0.0)
         nc.gpsimd.dma_start(
@@ -178,46 +183,51 @@ def tile_mix_sum_divided_by_drive_kernel(
         positive(1)
         square(0)
         inv_root(1)
+        cast(1, 0)
+        quantise(1, 0)
         wa_pass(0, 0, True, False)
-        wa_pass(1, 0, True, False)
+        wa_pass(0, 1, False, False)
+        wq_pass(0, 0, False, False)
+        wq_pass(0, 1, False, True)
         drive_tile(2)
         positive(2)
         square(1)
         inv_root(2)
-        cast(1, 0)
-        quantise(1, 0)
-        wa_pass(0, 1, False, False)
-        wq_pass(0, 0, False, False)
-        wq_pass(0, 1, False, True)
-        drive_tile(3)
-        positive(3)
-        square(2)
-        inv_root(3)
-        square(3)
+        wa_pass(1, 0, True, False)
         wa_pass(1, 1, False, False)
         wq_pass(1, 0, False, False)
         wq_pass(1, 1, False, True)
+        drive_tile(3)
+        positive(3)
+        square(2)
+        halves = (slice(0, T // 2), slice(T // 2, T))
+        for cols in halves:
+            inv_root(3, cols)
+        for cols in halves:
+            square(3, cols)
         for i in (2, 3):
             for z in range(PASSES):
                 wq_pass(i, z, z == 0, False)
 
-        divide(0)
         cast(0, 1)
-        add_share(0)
-        store(0)
+        divide(0)
         quantise(0, 1)
         wa_pass(2, 0, False, False)
         wa_pass(3, 0, False, False)
         cast(1, 1)
-        divide(1)
+        add_share(0)
+        store(0)
         quantise(1, 1)
         wa_pass(2, 1, False, True)
         wa_pass(3, 1, False, True)
+        divide(1)
+        divide(2)
         add_share(1)
         store(1)
-        divide(2)
-        divide(3)
         add_share(2)
         store(2)
-        add_share(3)
-        store(3)
+        for cols in halves:
+            divide(3, cols)
+        for cols in halves:
+            add_share(3, cols)
+            store(3, cols)

@@ -32,7 +32,7 @@ def tile_mix_sum_divided_by_drive_kernel(
         ctx.enter_context(tc.manual_schedule())
 
         xt_w = keep.tile([P, PASSES, T], U32, align_bytes=64)
-        wq_w = keep.tile([P, PASSES, N], U32, align_bytes=64)
+        wq_w = [keep.tile([P, PASSES, HALF], U32, name="wq_w%d" % h, align_bytes=64) for h in range(2)]
         xq_w = keep.tile([P, PASSES, 2 * T], U8, align_bytes=64)
         wd_w = keep.tile([P, PASSES, 2 * N], U8, align_bytes=64)
         staged = keep.tile([32, 4, PASSES, T], U8, align_bytes=64)
@@ -77,8 +77,8 @@ def tile_mix_sum_divided_by_drive_kernel(
 
         def cast(z, h):
             nc.vector.tensor_copy(
-                out=grouped[z, h][:].rearrange("p (c i) j -> p c j i", i=4),
-                in_=raw[z, h][:].rearrange("p j (c i) -> p c j i", i=4),
+                out=grouped[z, h][:],
+                in_=raw[z, h][:].rearrange("p j c -> p c j"),
             )
 
         def quantise(z, h):
@@ -112,9 +112,10 @@ def tile_mix_sum_divided_by_drive_kernel(
             )
 
         def wq_pass(i, z, start, stop):
+            h, c = divmod(i * P, HALF)
             nc.tensor.matmul_mx(
                 out=total[i][:],
-                lhsT=wq_w[:, z, P * i : P * (i + 1)].bitcast(FP8X4),
+                lhsT=wq_w[h][:, z, c : c + P].bitcast(FP8X4),
                 lhsT_scale=wq_s[:, z, P * i : P * (i + 1)],
                 rhs=xq_w[:, z, :].bitcast(FP4X4),
                 rhs_scale=xq_s[:, z, :],
@@ -158,76 +159,89 @@ def tile_mix_sum_divided_by_drive_kernel(
         nc.vector.memset(planes[:].rearrange("p a z c -> p (a z c)").bitcast(I32), 0)
         for a, scales in enumerate((xt_scales, wd_scales, xq_scales, wq_scales)):
             stage_scales(nc.scalar if a % 2 else nc.sync, a, scales)
-        load_wa(nc.scalar, 0, 0)
         load_fp8(nc.scalar, xt_w, xt_words)
         load_fp4(nc.scalar, wd_w, wd_words)
-        load_wa(nc.scalar, 1, 0)
+        load_wa(nc.scalar, 0, 0)
         place_scales()
-        load_fp4(nc.sync, xq_w, xq_words)
-        load_fp8(nc.sync, wq_w, wq_words)
+        load_wa(nc.sync, 1, 0)
         load_wa(nc.sync, 0, 1)
         load_wa(nc.sync, 1, 1)
+        load_fp4(nc.sync, xq_w, xq_words)
+        for h in range(2):
+            nc.sync.dma_start(
+                out=wq_w[h][:].bitcast(I32),
+                in_=wq_words[:, :, h * HALF : (h + 1) * HALF, :].rearrange("z p c r -> p z (c r)").bitcast(I32),
+            )
 
         def drive_tile(i):
             for z in range(PASSES):
                 drive_pass(i, z)
 
+        def sum_tile(i):
+            for z in range(PASSES):
+                wa_pass(i, z, z == 0, False)
+            for z in range(PASSES):
+                wq_pass(i, z, False, z == PASSES - 1)
+
+        warm_in = keep.tile([P, PACK * P], BF16, align_bytes=64)
+        warm_w = keep.tile([P, P], U32, align_bytes=64)
+        warm_s = keep.tile([P, P], U8, align_bytes=64)
+        nc.vector.memset(warm_in[:], 1.0)
+        nc.vector.quantize_mx(out=warm_w[:].bitcast(FP8X4), scales=warm_s[:], in_=warm_in[:])
+        for step in range(36):
+            nc.tensor.matmul_mx(
+                out=total[TILES - 1][:, 0:P],
+                lhsT=warm_w[:].bitcast(FP8X4),
+                lhsT_scale=warm_s[:],
+                rhs=warm_w[:].bitcast(FP8X4),
+                rhs_scale=warm_s[:],
+                start=True,
+                stop=True,
+            )
+
         cast(0, 0)
         quantise(0, 0)
         nc.vector.transpose(out=sh_cols[:], in_=sh_rows[:])
 
-        drive_tile(0)
-        drive_tile(1)
+        for i in range(TILES):
+            drive_tile(i)
         positive_v(0)
-        inv_root(0)
-        positive(1)
-        square(0)
-        inv_root(1)
-        cast(1, 0)
-        quantise(1, 0)
-        wa_pass(0, 0, True, False)
-        wa_pass(0, 1, False, False)
-        wq_pass(0, 0, False, False)
-        wq_pass(0, 1, False, True)
-        drive_tile(2)
-        positive(2)
-        square(1)
-        inv_root(2)
-        wa_pass(1, 0, True, False)
-        wa_pass(1, 1, False, False)
-        wq_pass(1, 0, False, False)
-        wq_pass(1, 1, False, True)
-        drive_tile(3)
-        positive(3)
-        square(2)
         halves = (slice(0, T // 2), slice(T // 2, T))
+        for i in range(TILES - 1):
+            inv_root(i)
+            positive(i + 1)
+            square(i)
         for cols in halves:
             inv_root(3, cols)
         for cols in halves:
             square(3, cols)
-        for i in (2, 3):
-            for z in range(PASSES):
-                wq_pass(i, z, z == 0, False)
 
+        cast(1, 0)
         cast(0, 1)
-        divide(0)
-        quantise(0, 1)
-        wa_pass(2, 0, False, False)
-        wa_pass(3, 0, False, False)
+        quantise(1, 0)
         cast(1, 1)
+        quantise(0, 1)
+        quantise(1, 1)
+        for z in range(PASSES):
+            for i in (0, 1):
+                wa_pass(i, z, z == 0, False)
+        for i in (0, 1):
+            for z in range(PASSES):
+                wq_pass(i, z, False, z == PASSES - 1)
+        sum_tile(2)
+        sum_tile(3)
+
+        divide(0)
+        divide(1)
         add_share(0)
         store(0)
-        quantise(1, 1)
-        wa_pass(2, 1, False, True)
-        wa_pass(3, 1, False, True)
-        divide(1)
-        divide(2)
         add_share(1)
         store(1)
+        divide(2)
+        divide(3, halves[0])
         add_share(2)
         store(2)
-        for cols in halves:
-            divide(3, cols)
+        divide(3, halves[1])
         for cols in halves:
             add_share(3, cols)
             store(3, cols)

from contextlib import ExitStack

import concourse.mybir as mybir

K, L, T, N = 1024, 1024, 512, 512
FLOPS = 2 * N * T * (K + L + K)

F32 = mybir.dt.float32
BF16 = mybir.dt.bfloat16
I32 = mybir.dt.int32
U32 = mybir.dt.uint32
U8 = mybir.dt.uint8
FP8X4 = mybir.dt.float8_e4m3fn_x4
FP4X4 = mybir.dt.float4_e2m1fn_x4
ACT = mybir.ActivationFunctionType
ALU = mybir.AluOpType

P = 128
PACK = 4
PASSES = 2
TILES = N // P
HALF = N // 2


def tile_mix_sum_divided_by_drive_kernel(
    tc, xt_words, xt_scales, wa, xq_words, xq_scales, wq_words, wq_scales, wd_words, wd_scales, sh, out
):
    nc = tc.nc
    with ExitStack() as ctx:
        keep = ctx.enter_context(tc.tile_pool(name="keep", bufs=1))
        psum = ctx.enter_context(tc.psum_pool(name="psum", bufs=1))
        ctx.enter_context(tc.manual_schedule())

        xt_w = keep.tile([P, PASSES, T], U32, align_bytes=64)
        wq_w = [keep.tile([P, PASSES, HALF], U32, name="wq_w%d" % h, align_bytes=64) for h in range(2)]
        xq_w = keep.tile([P, PASSES, 2 * T], U8, align_bytes=64)
        wd_w = keep.tile([P, PASSES, 2 * N], U8, align_bytes=64)
        staged = keep.tile([32, 4, PASSES, T], U8, align_bytes=64)
        planes = keep.tile([P, 4, PASSES, T], U8, align_bytes=64)
        xt_s, wd_s, xq_s, wq_s = (planes[:, a] for a in range(4))
        sh_rows = keep.tile([P, P], F32, align_bytes=64)
        sh_cols = keep.tile([P, P], F32, align_bytes=64)

        chunks = [(z, h) for h in range(2) for z in range(PASSES)]
        raw, grouped, wa_w, wa_s = {}, {}, {}, {}
        for z, h in chunks:
            raw[z, h] = keep.tile([P, PACK, HALF], F32, name="raw%d%d" % (z, h))
            grouped[z, h] = keep.tile([P, HALF, PACK], BF16, name="grouped%d%d" % (z, h), align_bytes=64)
            wa_w[z, h] = keep.tile([P, HALF], U32, name="wa_w%d%d" % (z, h), align_bytes=64)
            wa_s[z, h] = keep.tile([P, HALF], U8, name="wa_s%d%d" % (z, h), align_bytes=64)
        drive = [psum.tile([P, T], F32, name="drive%d" % i) for i in range(TILES)]
        total = [psum.tile([P, T], F32, name="total%d" % i) for i in range(TILES)]
        pos = [keep.tile([P, T], F32, name="pos%d" % i) for i in range(TILES)]
        root = [keep.tile([P, T], F32, name="root%d" % i) for i in range(TILES)]
        recip = [keep.tile([P, T], F32, name="recip%d" % i) for i in range(TILES)]
        quot = [keep.tile([P, T], F32, name="quot%d" % i) for i in range(TILES)]
        res = [keep.tile([P, T], F32, name="res%d" % i) for i in range(TILES)]

        def stage_scales(eng, a, scales):
            eng.dma_start(out=staged[16:32, a].bitcast(I32), in_=scales.rearrange("z q c -> q z c").bitcast(I32))

        def place_scales():
            src = staged[:].rearrange("p a z c -> p (a z c)").bitcast(I32)
            dst = planes[:].rearrange("p a z c -> p (a z c)").bitcast(I32)
            for r in range(4):
                nc.sync.dma_start(out=dst[r:P:32, :], in_=src[16 + r : 32 : 4, :])

        def load_fp8(eng, dst, words):
            eng.dma_start(out=dst[:].bitcast(I32), in_=words.rearrange("z p c r -> p z (c r)").bitcast(I32))

        def load_fp4(eng, dst, words):
            eng.dma_start(out=dst[:].bitcast(I32), in_=words.rearrange("z p c -> p z c").bitcast(I32))

        def load_wa(eng, z, h):
            rows = wa[z * 512 : (z + 1) * 512, h * HALF : (h + 1) * HALF]
            eng.dma_start(out=raw[z, h][:], in_=rows.rearrange("(p j) c -> p j c", j=PACK))

        def cast(z, h):
            nc.vector.tensor_copy(
                out=grouped[z, h][:],
                in_=raw[z, h][:].rearrange("p j c -> p c j"),
            )

        def quantise(z, h):
            nc.vector.quantize_mx(
                out=wa_w[z, h][:].bitcast(FP8X4),
                scales=wa_s[z, h][:],
                in_=grouped[z, h][:].rearrange("p c j -> p (c j)"),
            )

        def drive_pass(i, z):
            nc.tensor.matmul_mx(
                out=drive[i][:],
                lhsT=wd_w[:, z, 2 * P * i : 2 * P * (i + 1)].bitcast(FP4X4),
                lhsT_scale=wd_s[:, z, P * i : P * (i + 1)],
                rhs=xt_w[:, z, :].bitcast(FP8X4),
                rhs_scale=xt_s[:, z, :],
                start=(z == 0),
                stop=(z == PASSES - 1),
            )

        def wa_pass(i, z, start, stop):
            h, c = divmod(i * P, HALF)
            nc.tensor.matmul_mx(
                out=total[i][:],
                lhsT=wa_w[z, h][:, c : c + P].bitcast(FP8X4),
                lhsT_scale=wa_s[z, h][:, c : c + P],
                rhs=xt_w[:, z, :].bitcast(FP8X4),
                rhs_scale=xt_s[:, z, :],
                start=start,
                stop=stop,
            )

        def wq_pass(i, z, start, stop):
            h, c = divmod(i * P, HALF)
            nc.tensor.matmul_mx(
                out=total[i][:],
                lhsT=wq_w[h][:, z, c : c + P].bitcast(FP8X4),
                lhsT_scale=wq_s[:, z, P * i : P * (i + 1)],
                rhs=xq_w[:, z, :].bitcast(FP4X4),
                rhs_scale=xq_s[:, z, :],
                start=start,
                stop=stop,
            )

        def positive(i):
            nc.scalar.activation(out=pos[i][:], in_=drive[i][:], func=ACT.Relu)

        def positive_v(i):
            nc.vector.tensor_scalar(out=pos[i][:], in0=drive[i][:], scalar1=0.0, scalar2=None, op0=ALU.max)

        def inv_root(i, cols=slice(0, T)):
            nc.scalar.activation(out=root[i][:, cols], in_=pos[i][:, cols], func=ACT.Abs_reciprocal_sqrt, bias=1.0)

        def square(i, cols=slice(0, T)):
            nc.scalar.activation(out=recip[i][:, cols], in_=root[i][:, cols], func=ACT.Square)

        def divide(i, cols=slice(0, T)):
            nc.vector.tensor_tensor(out=quot[i][:, cols], in0=total[i][:, cols], in1=recip[i][:, cols], op=ALU.mult)

        def add_share(i, cols=slice(0, T)):
            nc.vector.scalar_tensor_tensor(
                out=res[i][:, cols],
                in0=drive[i][:, cols],
                scalar=sh_cols[:, 32 * i : 32 * i + 1],
                in1=quot[i][:, cols],
                op0=ALU.mult,
                op1=ALU.add,
            )

        def store(i, cols=slice(0, T)):
            nc.sync.dma_start(out=out[P * i : P * (i + 1), cols], in_=res[i][:, cols])

        nc.gpsimd.memset(sh_rows[:], 0.0)
        nc.gpsimd.dma_start(
            out=sh_rows[0:P:32, :].rearrange("a (i r) -> a i r", r=32),
            in_=sh.rearrange("(i a r) o -> a i (r o)", a=4, r=32),
        )
        nc.vector.memset(planes[:].rearrange("p a z c -> p (a z c)").bitcast(I32), 0)
        for a, scales in enumerate((xt_scales, wd_scales, xq_scales, wq_scales)):
            stage_scales(nc.scalar if a % 2 else nc.sync, a, scales)
        load_fp8(nc.scalar, xt_w, xt_words)
        load_fp4(nc.scalar, wd_w, wd_words)
        load_wa(nc.scalar, 0, 0)
        place_scales()
        load_wa(nc.sync, 1, 0)
        load_wa(nc.sync, 0, 1)
        load_wa(nc.sync, 1, 1)
        load_fp4(nc.sync, xq_w, xq_words)
        for h in range(2):
            nc.sync.dma_start(
                out=wq_w[h][:].bitcast(I32),
                in_=wq_words[:, :, h * HALF : (h + 1) * HALF, :].rearrange("z p c r -> p z (c r)").bitcast(I32),
            )

        def drive_tile(i):
            for z in range(PASSES):
                drive_pass(i, z)

        def sum_tile(i):
            for z in range(PASSES):
                wa_pass(i, z, z == 0, False)
            for z in range(PASSES):
                wq_pass(i, z, False, z == PASSES - 1)

        warm_in = keep.tile([P, PACK * P], BF16, align_bytes=64)
        warm_w = keep.tile([P, P], U32, align_bytes=64)
        warm_s = keep.tile([P, P], U8, align_bytes=64)
        nc.vector.memset(warm_in[:], 1.0)
        nc.vector.quantize_mx(out=warm_w[:].bitcast(FP8X4), scales=warm_s[:], in_=warm_in[:])
        for step in range(36):
            nc.tensor.matmul_mx(
                out=total[TILES - 1][:, 0:P],
                lhsT=warm_w[:].bitcast(FP8X4),
                lhsT_scale=warm_s[:],
                rhs=warm_w[:].bitcast(FP8X4),
                rhs_scale=warm_s[:],
                start=True,
                stop=True,
            )

        cast(0, 0)
        quantise(0, 0)
        nc.vector.transpose(out=sh_cols[:], in_=sh_rows[:])

        for i in range(TILES):
            drive_tile(i)
        positive_v(0)
        halves = (slice(0, T // 2), slice(T // 2, T))
        for i in range(TILES - 1):
            inv_root(i)
            positive(i + 1)
            square(i)
        for cols in halves:
            inv_root(3, cols)
        for cols in halves:
            square(3, cols)

        cast(1, 0)
        cast(0, 1)
        quantise(1, 0)
        cast(1, 1)
        quantise(0, 1)
        quantise(1, 1)
        for z in range(PASSES):
            for i in (0, 1):
                wa_pass(i, z, z == 0, False)
        for i in (0, 1):
            for z in range(PASSES):
                wq_pass(i, z, False, z == PASSES - 1)
        sum_tile(2)
        sum_tile(3)

        divide(0)
        divide(1)
        add_share(0)
        store(0)
        add_share(1)
        store(1)
        divide(2)
        divide(3, halves[0])
        add_share(2)
        store(2)
        divide(3, halves[1])
        for cols in halves:
            add_share(3, cols)
            store(3, cols)
